import numpy as np
import ml_dtypes


def mxq(x, axis, fmt="e4m3"):
    dtype, down = {"e4m3": (ml_dtypes.float8_e4m3fn, 7), "e5m2": (ml_dtypes.float8_e5m2, 14)}[fmt]
    v = np.moveaxis(np.asarray(x, np.float32).astype(ml_dtypes.bfloat16).astype(np.float64), axis, -1)
    blocks = v.reshape(v.shape[:-1] + (-1, 32))
    amax = np.abs(blocks).max(-1, keepdims=True)
    byte = np.maximum(np.where(amax > 0, np.frexp(amax)[1] - 1 + 127, 0) - down, 1)
    scale = np.exp2(byte - 127.0)
    codes = (blocks / scale).astype(np.float32).astype(dtype).astype(np.float64)
    return np.moveaxis((codes * scale).reshape(v.shape), -1, axis)


WIDE = False


def mx_kscale(k):
    if not WIDE:
        return np.ones(k)
    levels = np.array([10, -10, 5, -5, 0])
    if k % 512:
        return np.exp2(np.random.permutation(np.resize(levels, k // 32))).repeat(32)
    a = np.empty((k // 512, 16))
    for p in range(k // 512):
        a[p, :8] = np.random.permutation(np.resize(levels, 8))
        for g in range(8):
            far = levels[np.abs(levels - a[p, g]) >= 10]
            a[p, g + 8] = far[np.random.randint(len(far))]
    return np.exp2(a.ravel()).repeat(32)


def f64(x):
    return np.asarray(x).astype(np.float64)


def striped(idx):
    return np.tile(np.asarray(idx).reshape(-1, 16).T, (8, 1)).astype(np.uint16)


def unstriped(offs):
    return offs[:16].T.reshape(-1).astype(np.int64)


E2M1 = np.array([0.0, 0.5, 1.0, 1.5, 2.0, 3.0, 4.0, 6.0, -0.0, -0.5, -1.0, -1.5, -2.0, -3.0, -4.0, -6.0])


def pack_weight(w, fmt):
    k, n = w.shape
    w = f64(np.asarray(w, np.float32).astype(ml_dtypes.bfloat16)).reshape(k // 32, 32, n)
    amax = np.abs(w).max(1)
    if fmt == "e4m3":
        byte = np.frexp(amax)[1] - 1 + 127 - 7
    else:
        mant, ex = np.frexp(amax / 6.0)
        byte = np.where(mant > 0.5, ex, ex - 1) + 127
    byte = np.clip(np.where(amax > 0, byte, 1), 1, 254)
    scaled = (w * np.exp2(127.0 - byte)[:, None, :]).reshape(k, n).astype(np.float32)
    by_word = np.ascontiguousarray(scaled.reshape(k // 512, 128, 4, n).transpose(0, 1, 3, 2))
    if fmt == "e4m3":
        words = by_word.astype(ml_dtypes.float8_e4m3fn).view(np.uint8)
    else:
        c = by_word.astype(ml_dtypes.float4_e2m1fn).view(np.uint8) & 0xF
        words = (c[..., 0::2] | (c[..., 1::2] << 4)).reshape(k // 512, 128, 2 * n)
    return np.ascontiguousarray(words), np.ascontiguousarray(byte.astype(np.uint8).reshape(k // 512, 16, n))


def unpack_weight(words, scales, fmt):
    g, _, n = scales.shape
    words = np.ascontiguousarray(words).reshape(g, 128, n, -1)
    if fmt == "e4m3":
        vals = words.view(ml_dtypes.float8_e4m3fn).astype(np.float64)
    else:
        nib = np.empty((g, 128, n, 4), np.uint8)
        nib[..., 0::2] = words & 0xF
        nib[..., 1::2] = words >> 4
        vals = E2M1[nib]
    vals = vals * np.repeat(np.exp2(scales.astype(np.float64) - 127.0), 8, axis=1)[..., None]
    return vals.transpose(0, 1, 3, 2).reshape(g * 512, n)


def softplus(v):
    return np.log(1.0 + np.exp(v))


def sigmoid(v):
    return 1.0 / (1.0 + np.exp(-v))


K, R, F, T, J, M = 512, 128, 512, 2048, 512, 256


def setup_inputs():
    n = np.random.standard_normal
    idx = np.random.permutation(T)[:J]
    idx2 = np.random.permutation(J)[:M]
    idx3 = np.random.permutation(J)[:M]
    idx4 = np.random.permutation(J)[:M]
    fk = mx_kscale(K)
    ff = mx_kscale(F)
    fj = mx_kscale(J)
    tj = np.ones(T)
    tj[idx] = fj
    tabp = pack_weight(n((K, T)) / fk[:, None], "e2m1")
    return {
        "tab_words": tabp[0],
        "tab_scales": tabp[1],
        "w1": (n((K, R)) * 1 / np.sqrt(K) * fk[:, None]).astype(np.float32),
        "bias": (np.random.uniform(-0.5, 0.5, (R, 1))).astype(np.float32),
        "wo": (n((F, R)) * 1 / np.sqrt(F) * ff[:, None]).astype(np.float32),
        "dy": (n((F, M)) / ff[:, None]).astype(np.float32),
        "js": (np.random.uniform(0.5, 2.0, (1, J)) * fj).astype(np.float32),
        "xrows": (n((K, T)) / tj).astype(np.float32),
        "old": (n((K, R)) * 4.0).astype(np.float32),
        "offs": striped(idx),
        "offs2": striped(idx2),
        "offs3": striped(idx3),
        "offs4": striped(idx4),
    }


def reference(tab_words, tab_scales, w1, bias, wo, dy, js, xrows, old, offs, offs2, offs3, offs4):
    idx = unstriped(offs)
    idx2 = unstriped(offs2)
    idx3 = unstriped(offs3)
    idx4 = unstriped(offs4)
    tabu = unpack_weight(tab_words, tab_scales, "e2m1")
    w1q = mxq(f64(w1), 0, "e4m3")
    tabidxg = tabu[:, idx]
    a = w1q.T @ tabidxg
    h1 = softplus(a + f64(bias))
    s = h1[:, idx2] * h1[:, idx3] * h1[:, idx4]
    woq = mxq(f64(wo), 0, "e4m3")
    dyq = mxq(f64(dy), 0, "e4m3")
    c0 = woq.T @ dyq
    ds = c0 / (s + 1.0)
    e1 = ds * h1[:, idx4] * h1[:, idx3]
    s1 = np.zeros((R, J))
    s1[:, idx2] = e1
    e2 = ds * h1[:, idx4] * h1[:, idx2]
    s2 = np.zeros((R, J))
    s2[:, idx3] = e2
    e3 = ds * h1[:, idx2] * h1[:, idx3]
    s3 = np.zeros((R, J))
    s3[:, idx4] = e3
    dh1 = s1 + s2 + s3
    da = dh1 * sigmoid(a + f64(bias))
    gs = da * f64(js)
    gt1 = gs.T
    xt = f64(xrows)[:, idx].T
    xtq = mxq(xt, 0, "e4m3")
    gt1q = mxq(gt1, 0, "e4m3")
    gw = xtq.T @ gt1q
    y = gw + f64(old)
    return y

@@ -1,0 +1,219 @@
+from contextlib import ExitStack
+
+import concourse.mybir as mybir
+from concourse.masks import make_identity
+
+K, R, F, T, J, M = 512, 128, 512, 2048, 512, 256
+FLOPS = 2 * K * R * J + 2 * F * R * M + 2 * J * K * R
+
+F32 = mybir.dt.float32
+BF16 = mybir.dt.bfloat16
+I32 = mybir.dt.int32
+U32 = mybir.dt.uint32
+U16 = mybir.dt.uint16
+U8 = mybir.dt.uint8
+FP8X4 = mybir.dt.float8_e4m3fn_x4
+FP4X4 = mybir.dt.float4_e2m1fn_x4
+ACT = mybir.ActivationFunctionType
+ALU = mybir.AluOpType
+
+P = 128
+PACK = 4
+HALF = J // 2
+EZ_AT = 0
+X1_AT = EZ_AT + 8 * J
+PLACED_AT = X1_AT + 4 * T
+JS_AT = PLACED_AT + 4 * J + 4 * M
+DY_AT = JS_AT + 2 * T
+H_AT = DY_AT + 16 * M
+S_AT = H_AT + 4 * T
+
+
+def tile_attend_ctriples_w_kernel(tc, tab_words, tab_scales, w1, bias, wo, dy, js, xrows, old,
+                                   offs, offs2, offs3, offs4, out):
+    nc = tc.nc
+    with ExitStack() as ctx:
+        sb = ctx.enter_context(tc.tile_pool(name="sb", bufs=1))
+        hold = ctx.enter_context(tc.tile_pool(name="hold", bufs=1))
+        ps = ctx.enter_context(tc.psum_pool(name="ps", bufs=1))
+
+        def held(name, width, dtype, at):
+            return hold.tile([P, width], dtype, name=name, offset=at, align_bytes=64)
+
+        def quantize(name, src, scales):
+            codes = sb.tile([P, src.shape[1] // PACK], U32, name=name, align_bytes=64)
+            nc.vector.quantize_mx(out=codes[:].bitcast(FP8X4), scales=scales[:], in_=src)
+            return codes
+
+        def interleave(grouped, raw):
+            nc.scalar.activation(grouped.rearrange("p (c i t) -> p c t i", i=4, t=PACK),
+                                 raw[:].rearrange("p t (c i) -> p c t i", i=4), ACT.Copy)
+
+        def turn_x(xg, bank, xt):
+            pairs = xg[:].bitcast(F32)
+            for u in range(2):
+                nc.tensor.transpose(bank[:, u, :], pairs[:, u:J // 2:2], ident[:])
+            nc.scalar.copy(xt.bitcast(F32).rearrange("p (k u) -> p k u", u=2), bank[:].rearrange("p u k -> p k u"))
+
+        idx = sb.tile([P, J // 16], U16, name="idx")
+        nc.sync.dma_start(idx[:], offs)
+        words = sb.tile([P, T], U16, name="words", align_bytes=64)
+        nc.sync.dma_start(words[:].bitcast(I32), tab_words[0].bitcast(I32))
+        b_col = sb.tile([P, 1], F32, name="b_col")
+        nc.sync.dma_start(b_col[:], bias)
+        w1_raw = sb.tile([P, PACK, R], F32, name="w1_raw")
+        nc.sync.dma_start(w1_raw[:], w1.rearrange("(p t) r -> p t r", t=PACK))
+        sbytes = sb.tile([P, T], U8, name="sbytes", align_bytes=64)
+        nc.gpsimd.memset(sbytes[:].bitcast(I32), 0)
+        for q in range(4):
+            nc.sync.dma_start(sbytes[32 * q:32 * q + 4, :].bitcast(I32),
+                              tab_scales[0, 4 * q:4 * q + 4, :].bitcast(I32))
+        x_rows = xrows.rearrange("(p c) t -> p c t", c=PACK)
+        x_win = [held("x_win0", T, F32, H_AT), held("x_win1", T, F32, X1_AT),
+                 sb.tile([P, T], F32, name="x_win2", tag="x2", align_bytes=64), sb.tile([P, T], F32, name="x_win3")]
+        nc.sync.dma_start(x_win[0][:], x_rows[:, 0, :])
+        lists = []
+        for n, src in enumerate((offs2, offs3, offs4)):
+            lst = sb.tile([P, M // 16], U16, name=f"idx{n + 2}")
+            nc.sync.dma_start(lst[:], src)
+            lists.append(lst)
+        wo_raw = sb.tile([P, PACK, R], F32, name="wo_raw")
+        nc.sync.dma_start(wo_raw[:], wo.rearrange("(p t) r -> p t r", t=PACK))
+        dy_raw = hold.tile([P, PACK, M], F32, name="dy_raw", offset=DY_AT, align_bytes=64)
+        nc.sync.dma_start(dy_raw[:], dy.rearrange("(p t) m -> p t m", t=PACK))
+        js_col = sb.tile([P, PACK], F32, name="js_col")
+        nc.sync.dma_start(js_col[:], js.rearrange("o (p t) -> (o p) t", t=PACK))
+        nc.sync.dma_start(x_win[1][:], x_rows[:, 1, :])
+        nc.sync.dma_start(x_win[3][:], x_rows[:, 3, :])
+        nc.sync.dma_start(x_win[2][:], x_rows[:, 2, :])
+        old_sb = sb.tile([P, PACK * R], F32, name="old_sb")
+        nc.sync.dma_start(old_sb[:], old.rearrange("(p c) r -> p (c r)", c=PACK))
+
+        ident = sb.tile([P, P], F32, name="ident")
+        make_identity(nc, ident[:])
+        placed = [sb.tile([P, J], F32, name="placed0"), held("placed1", J, F32, PLACED_AT),
+                  sb.tile([P, J], F32, name="placed2")]
+        for win in placed:
+            nc.vector.memset(win[:], 0.0)
+        half_b = sb.tile([P, 1], F32, name="half_b")
+        nc.gpsimd.tensor_scalar(half_b[:], b_col[:], 0.5, 0.0, ALU.mult, ALU.add)
+        half_js = held("half_js", PACK, F32, JS_AT)
+        nc.gpsimd.tensor_scalar(half_js[:], js_col[:], 0.5, 0.0, ALU.mult, ALU.add)
+
+        w1_bf = sb.tile([P, R * PACK], BF16, name="w1_bf", align_bytes=64)
+        interleave(w1_bf[:], w1_raw)
+        tab_w = sb.tile([P, J], U16, name="tab_w", align_bytes=64)
+        nc.vector.tensor_copy(tab_w[:], words[:].indirect(idx[:]))
+        w1_scales = sb.tile([P, R], U8, name="w1_scales", align_bytes=64)
+        w1_codes = quantize("w1_codes", w1_bf[:], w1_scales)
+        a_ps = []
+        ez = held("ez", J, F32, EZ_AT)
+        for u in range(2):
+            tab_s = sb.tile([P, HALF], U8, name=f"tab_s{u}", align_bytes=64)
+            nc.vector.tensor_copy(tab_s[:], sbytes[:].indirect(idx[:, u * HALF // 16:(u + 1) * HALF // 16]))
+            acc = ps.tile([P, HALF], F32, name=f"a_ps{u}")
+            nc.tensor.matmul_mx(out=acc[:], lhsT=w1_codes[:].bitcast(FP8X4), lhsT_scale=w1_scales[:],
+                                rhs=tab_w[:, u * HALF:(u + 1) * HALF].bitcast(FP4X4), rhs_scale=tab_s[:],
+                                start=True, stop=True)
+            a_ps.append(acc)
+            mag = sb.tile([P, HALF], F32, name=f"mag{u}", tag=f"mag{u}")
+            nc.scalar.activation(mag[:], acc[:], ACT.Abs, bias=b_col[:])
+            nc.scalar.activation(ez[:, u * HALF:(u + 1) * HALF], mag[:], ACT.Exp, scale=-1.0)
+
+        pos = []
+        for u in range(2):
+            r = sb.tile([P, HALF], F32, name=f"pos{u}")
+            nc.vector.tensor_scalar(r[:], a_ps[u][:], b_col[:], 0.0, ALU.add, ALU.max)
+            pos.append(r)
+        xg0 = sb.tile([P, J], BF16, name="xg0", align_bytes=64)
+        nc.vector.tensor_copy(xg0[:], x_win[0][:].indirect(idx[:]))
+        h = held("h", J, F32, H_AT)
+        for u in range(2):
+            soft = sb.tile([P, HALF], F32, name=f"soft{u}", tag=f"mag{1 - u}")
+            nc.scalar.activation(soft[:], ez[:, u * HALF:(u + 1) * HALF], ACT.Ln, bias=1.0)
+            nc.vector.tensor_tensor(h[:, u * HALF:(u + 1) * HALF], soft[:], pos[u][:], ALU.add)
+
+        early = held("early", 4 * J, BF16, EZ_AT)
+        turn_x(xg0, ps.tile([P, 2, P], F32, name="x_ps0", tag="x_ps"), early[:, 0:J])
+        interleave(early[:, J:2 * J], wo_raw)
+        interleave(early[:, 2 * J:4 * J], dy_raw)
+
+        g2, g3, g4 = (sb.tile([P, M], F32, name=f"g{n}") for n in (2, 3, 4))
+        for g, lst in zip((g2, g3, g4), lists):
+            nc.vector.tensor_copy(g[:], h[:].indirect(lst[:]))
+        p23 = sb.tile([P, M], F32, name="p23")
+        nc.vector.tensor_tensor(p23[:], g2[:], g3[:], ALU.mult)
+        s = held("s", M, F32, S_AT)
+        nc.vector.tensor_tensor(s[:], p23[:], g4[:], ALU.mult)
+        early_scales = held("early_scales", J, U8, H_AT)
+        early_codes = quantize("early_codes", early[:], early_scales)
+        c0 = ps.tile([P, M], F32, name="c0")
+        nc.tensor.matmul_mx(out=c0[:], lhsT=early_codes[:, P:2 * P].bitcast(FP8X4), lhsT_scale=early_scales[:, P:2 * P],
+                            rhs=early_codes[:, 2 * P:4 * P].bitcast(FP8X4), rhs_scale=early_scales[:, 2 * P:4 * P],
+                            start=True, stop=True)
+        lns = held("lns", M, F32, DY_AT + 6 * M)
+        nc.scalar.activation(lns[:], s[:], ACT.Ln, bias=1.0)
+        rec = sb.tile([P, M], F32, name="rec")
+        nc.scalar.activation(rec[:], lns[:], ACT.Exp, scale=-1.0)
+        xg1 = held("xg1", J, BF16, S_AT)
+        nc.vector.tensor_copy(xg1[:], x_win[1][:].indirect(idx[:]))
+        cg4 = held("cg4", M, F32, X1_AT)
+        nc.vector.tensor_tensor(cg4[:], c0[:], g4[:], ALU.mult)
+        q3 = held("q3", M, F32, PLACED_AT - 4 * M)
+        nc.vector.tensor_tensor(q3[:], c0[:], p23[:], ALU.mult)
+        q1 = sb.tile([P, M], F32, name="q1")
+        nc.vector.tensor_tensor(q1[:], cg4[:], g3[:], ALU.mult)
+        q2 = sb.tile([P, M], F32, name="q2")
+        nc.vector.tensor_tensor(q2[:], cg4[:], g2[:], ALU.mult)
+
+        th = held("th", J, F32, DY_AT)
+        for u in range(2):
+            nc.scalar.activation(th[:, u * HALF:(u + 1) * HALF], a_ps[u][:], ACT.Tanh, bias=half_b[:], scale=0.5)
+        th_ps = ps.tile([P, PACK, R], F32, name="th_ps", tag="turned")
+        for t in range(PACK):
+            nc.tensor.transpose(th_ps[:, t, :], th[:, t:J:PACK], ident[:])
+        mid = held("mid", 2 * J, BF16, DY_AT + 8 * M)
+        turn_x(xg1, ps.tile([P, 2, P], F32, name="x_ps1", tag="x_ps"), mid[:, 0:J])
+        sj = sb.tile([P, PACK, R], F32, name="sj")
+        for t in range(PACK):
+            nc.scalar.activation(sj[:, t, :], th_ps[:, t, :], ACT.Identity,
+                                 bias=half_js[:, t:t + 1], scale=half_js[:, t:t + 1])
+        x3_bf = held("x3_bf", T, BF16, JS_AT)
+        nc.scalar.activation(x3_bf[:], x_win[3][:], ACT.Copy)
+
+        dh_ps = ps.tile([P, PACK, R], F32, name="dh_ps", tag="turned")
+        for n, (win, lst, qn) in enumerate(zip(placed, lists, (q1, q2, q3))):
+            nc.vector.tensor_tensor(win[:].indirect(lst[:]), qn[:], rec[:], ALU.mult)
+            for t in range(PACK):
+                nc.tensor.matmul(dh_ps[:, t, :], lhsT=win[:, t:J:PACK], rhs=ident[:], is_transpose=True,
+                                 start=(n == 0 and t == 0), stop=(n == 2 and t == PACK - 1))
+        xg3 = held("xg3", J, BF16, PLACED_AT + 2 * J)
+        nc.scalar.activation(xg3[:], x3_bf[:].indirect(idx[:]), ACT.Copy)
+        turn_x(xg3, ps.tile([P, 2, P], F32, name="x_ps3"), mid[:, J:2 * J])
+        xg2 = held("xg2", J, BF16, PLACED_AT - J)
+        nc.vector.tensor_copy(xg2[:], x_win[2][:].indirect(idx[:]))
+        xt2 = held("xt2", J, BF16, JS_AT)
+        turn_x(xg2, ps.tile([P, 2, P], F32, name="x_ps2", tag="x_ps"), xt2[:])
+
+        gs = sb.tile([P, R * PACK], BF16, name="gs", tag="x2", align_bytes=64)
+        nc.vector.tensor_tensor(gs[:].rearrange("p (c i t) -> p c t i", i=4, t=PACK),
+                                dh_ps[:].rearrange("p t (c i) -> p c t i", i=4),
+                                sj[:].rearrange("p t (c i) -> p c t i", i=4), ALU.mult)
+        late = {}
+        for name, src in (("mid", mid), ("g", gs), ("x2", xt2)):
+            scales = sb.tile([P, src.shape[1] // PACK], U8, name=name + "_scales", align_bytes=64)
+            late[name] = (quantize(name + "_codes", src[:], scales)[:], scales[:])
+        xq = [(early_codes[:, 0:P], early_scales[:, 0:P]), (late["mid"][0][:, 0:P], late["mid"][1][:, 0:P]), late["x2"],
+              (late["mid"][0][:, P:2 * P], late["mid"][1][:, P:2 * P])]
+        g_codes, g_scales = late["g"]
+        res = sb.tile([P, PACK * R], F32, name="res")
+        out_rows = out.rearrange("(p c) r -> p (c r)", c=PACK)
+        for u, queue in enumerate((nc.sync, nc.scalar)):
+            gw = ps.tile([P, 2 * R], F32, name=f"gw{u}")
+            for c in range(2):
+                codes, scales = xq[2 * u + c]
+                nc.tensor.matmul_mx(out=gw[:, c * R:(c + 1) * R], lhsT=codes.bitcast(FP8X4), lhsT_scale=scales,
+                                    rhs=g_codes.bitcast(FP8X4), rhs_scale=g_scales, start=True, stop=True)
+            cols = slice(u * 2 * R, (u + 1) * 2 * R)
+            nc.vector.tensor_tensor(res[:, cols], gw[:], old_sb[:, cols], ALU.add)
+            queue.dma_start(out_rows[:, cols], res[:, cols])

@@ -1,3 +1,4 @@
+import math
 from contextlib import ExitStack
 
 import concourse.mybir as mybir
@@ -20,13 +21,16 @@ ALU = mybir.AluOpType
 P = 128
 PACK = 4
 HALF = J // 2
-EZ_AT = 0
-X1_AT = EZ_AT + 8 * J
-PLACED_AT = X1_AT + 4 * T
-JS_AT = PLACED_AT + 4 * J + 4 * M
+EZ_AT = 2 * J
+PLACED_AT = EZ_AT + 4 * J
+JS_AT = PLACED_AT + 4 * J
 DY_AT = JS_AT + 2 * T
-H_AT = DY_AT + 16 * M
-S_AT = H_AT + 4 * T
+X0_AT = DY_AT + 16 * M
+MAG_AT = X0_AT + 4 * T
+POS_AT = MAG_AT - 2 * J
+SOFT_AT = MAG_AT + 2 * J
+H_AT = SOFT_AT + 4 * J
+X2_AT = H_AT + 4 * T
 
 
 def tile_attend_ctriples_w_kernel(tc, tab_words, tab_scales, w1, bias, wo, dy, js, xrows, old,
@@ -69,23 +73,23 @@ def tile_attend_ctriples_w_kernel(tc, tab_words, tab_scales, w1, bias, wo, dy, j
             nc.sync.dma_start(sbytes[32 * q:32 * q + 4, :].bitcast(I32),
                               tab_scales[0, 4 * q:4 * q + 4, :].bitcast(I32))
         x_rows = xrows.rearrange("(p c) t -> p c t", c=PACK)
-        x_win = [held("x_win0", T, F32, H_AT), held("x_win1", T, F32, X1_AT),
-                 sb.tile([P, T], F32, name="x_win2", tag="x2", align_bytes=64), sb.tile([P, T], F32, name="x_win3")]
+        x_win = [held("x_win0", T, F32, X0_AT), held("x_win1", T, F32, H_AT),
+                 held("x_win2", T, F32, X2_AT), sb.tile([P, T], F32, name="x_win3")]
         nc.sync.dma_start(x_win[0][:], x_rows[:, 0, :])
+        nc.sync.dma_start(x_win[1][:], x_rows[:, 1, :])
         lists = []
         for n, src in enumerate((offs2, offs3, offs4)):
             lst = sb.tile([P, M // 16], U16, name=f"idx{n + 2}")
             nc.sync.dma_start(lst[:], src)
             lists.append(lst)
-        wo_raw = sb.tile([P, PACK, R], F32, name="wo_raw")
-        nc.sync.dma_start(wo_raw[:], wo.rearrange("(p t) r -> p t r", t=PACK))
         dy_raw = hold.tile([P, PACK, M], F32, name="dy_raw", offset=DY_AT, align_bytes=64)
         nc.sync.dma_start(dy_raw[:], dy.rearrange("(p t) m -> p t m", t=PACK))
-        js_col = sb.tile([P, PACK], F32, name="js_col")
+        wo_raw = sb.tile([P, PACK, R], F32, name="wo_raw", tag="wo", align_bytes=64)
+        nc.sync.dma_start(wo_raw[:], wo.rearrange("(p t) r -> p t r", t=PACK))
+        js_col = held("js_col", PACK, F32, JS_AT)
         nc.sync.dma_start(js_col[:], js.rearrange("o (p t) -> (o p) t", t=PACK))
-        nc.sync.dma_start(x_win[1][:], x_rows[:, 1, :])
-        nc.sync.dma_start(x_win[3][:], x_rows[:, 3, :])
         nc.sync.dma_start(x_win[2][:], x_rows[:, 2, :])
+        nc.sync.dma_start(x_win[3][:], x_rows[:, 3, :])
         old_sb = sb.tile([P, PACK * R], F32, name="old_sb")
         nc.sync.dma_start(old_sb[:], old.rearrange("(p c) r -> p (c r)", c=PACK))
 
@@ -97,8 +101,6 @@ def tile_attend_ctriples_w_kernel(tc, tab_words, tab_scales, w1, bias, wo, dy, j
             nc.vector.memset(win[:], 0.0)
         half_b = sb.tile([P, 1], F32, name="half_b")
         nc.gpsimd.tensor_scalar(half_b[:], b_col[:], 0.5, 0.0, ALU.mult, ALU.add)
-        half_js = held("half_js", PACK, F32, JS_AT)
-        nc.gpsimd.tensor_scalar(half_js[:], js_col[:], 0.5, 0.0, ALU.mult, ALU.add)
 
         w1_bf = sb.tile([P, R * PACK], BF16, name="w1_bf", align_bytes=64)
         interleave(w1_bf[:], w1_raw)
@@ -108,58 +110,63 @@ def tile_attend_ctriples_w_kernel(tc, tab_words, tab_scales, w1, bias, wo, dy, j
         w1_codes = quantize("w1_codes", w1_bf[:], w1_scales)
         a_ps = []
         ez = held("ez", J, F32, EZ_AT)
+        mag = held("mag", J, F32, MAG_AT)
+        halves = [slice(u * HALF, (u + 1) * HALF) for u in range(2)]
         for u in range(2):
             tab_s = sb.tile([P, HALF], U8, name=f"tab_s{u}", align_bytes=64)
             nc.vector.tensor_copy(tab_s[:], sbytes[:].indirect(idx[:, u * HALF // 16:(u + 1) * HALF // 16]))
-            acc = ps.tile([P, HALF], F32, name=f"a_ps{u}")
+            acc = ps.tile([P, HALF], F32, name=f"a_ps{u}", tag=f"a{u}")
             nc.tensor.matmul_mx(out=acc[:], lhsT=w1_codes[:].bitcast(FP8X4), lhsT_scale=w1_scales[:],
                                 rhs=tab_w[:, u * HALF:(u + 1) * HALF].bitcast(FP4X4), rhs_scale=tab_s[:],
                                 start=True, stop=True)
             a_ps.append(acc)
-            mag = sb.tile([P, HALF], F32, name=f"mag{u}", tag=f"mag{u}")
-            nc.scalar.activation(mag[:], acc[:], ACT.Abs, bias=b_col[:])
-            nc.scalar.activation(ez[:, u * HALF:(u + 1) * HALF], mag[:], ACT.Exp, scale=-1.0)
+            nc.scalar.activation(mag[:, halves[u]], acc[:], ACT.Abs, bias=b_col[:])
+            nc.scalar.activation(ez[:, halves[u]], mag[:, halves[u]], ACT.Exp, scale=-1.0)
 
-        pos = []
-        for u in range(2):
-            r = sb.tile([P, HALF], F32, name=f"pos{u}")
-            nc.vector.tensor_scalar(r[:], a_ps[u][:], b_col[:], 0.0, ALU.add, ALU.max)
-            pos.append(r)
         xg0 = sb.tile([P, J], BF16, name="xg0", align_bytes=64)
         nc.vector.tensor_copy(xg0[:], x_win[0][:].indirect(idx[:]))
-        h = held("h", J, F32, H_AT)
+        pos = held("pos", J, F32, POS_AT)
         for u in range(2):
-            soft = sb.tile([P, HALF], F32, name=f"soft{u}", tag=f"mag{1 - u}")
-            nc.scalar.activation(soft[:], ez[:, u * HALF:(u + 1) * HALF], ACT.Ln, bias=1.0)
-            nc.vector.tensor_tensor(h[:, u * HALF:(u + 1) * HALF], soft[:], pos[u][:], ALU.add)
+            nc.vector.tensor_scalar(pos[:, halves[u]], a_ps[u][:], b_col[:], 0.0, ALU.add, ALU.max)
+        xg1 = sb.tile([P, J], BF16, name="xg1", align_bytes=64)
+        nc.vector.tensor_copy(xg1[:], x_win[1][:].indirect(idx[:]))
+        h = held("h", J, F32, H_AT)
+        soft = held("soft", J, F32, SOFT_AT)
+        for u in range(2):
+            nc.scalar.activation(soft[:, halves[u]], ez[:, halves[u]], ACT.Ln, bias=1.0)
+            nc.vector.tensor_tensor(h[:, halves[u]], soft[:, halves[u]], pos[:, halves[u]], ALU.add)
 
-        early = held("early", 4 * J, BF16, EZ_AT)
-        turn_x(xg0, ps.tile([P, 2, P], F32, name="x_ps0", tag="x_ps"), early[:, 0:J])
-        interleave(early[:, J:2 * J], wo_raw)
-        interleave(early[:, 2 * J:4 * J], dy_raw)
+        dy_bf = held("dy_bf", 2 * J, BF16, EZ_AT - 2 * J)
+        interleave(dy_bf[:], dy_raw)
+        wo_bf = held("wo_bf", J, BF16, EZ_AT + 2 * J)
+        interleave(wo_bf[:], wo_raw)
+        xt01 = sb.tile([P, 2 * J], BF16, name="xt01", tag="wo", align_bytes=64)
+        turn_x(xg0, ps.tile([P, 2, P], F32, name="x_ps0", tag="x_ps"), xt01[:, 0:J])
+        turn_x(xg1, ps.tile([P, 2, P], F32, name="x_ps1"), xt01[:, J:2 * J])
 
         g2, g3, g4 = (sb.tile([P, M], F32, name=f"g{n}") for n in (2, 3, 4))
         for g, lst in zip((g2, g3, g4), lists):
             nc.vector.tensor_copy(g[:], h[:].indirect(lst[:]))
         p23 = sb.tile([P, M], F32, name="p23")
         nc.vector.tensor_tensor(p23[:], g2[:], g3[:], ALU.mult)
-        s = held("s", M, F32, S_AT)
+        dy_scales = held("dy_scales", M, U8, H_AT)
+        dy_codes = quantize("dy_codes", dy_bf[:], dy_scales)
+        s = sb.tile([P, M], F32, name="s")
         nc.vector.tensor_tensor(s[:], p23[:], g4[:], ALU.mult)
-        early_scales = held("early_scales", J, U8, H_AT)
-        early_codes = quantize("early_codes", early[:], early_scales)
+        wo_scales = held("wo_scales", R, U8, EZ_AT)
+        wo_codes = quantize("wo_codes", wo_bf[:], wo_scales)
         c0 = ps.tile([P, M], F32, name="c0")
-        nc.tensor.matmul_mx(out=c0[:], lhsT=early_codes[:, P:2 * P].bitcast(FP8X4), lhsT_scale=early_scales[:, P:2 * P],
-                            rhs=early_codes[:, 2 * P:4 * P].bitcast(FP8X4), rhs_scale=early_scales[:, 2 * P:4 * P],
-                            start=True, stop=True)
+        nc.tensor.matmul_mx(out=c0[:], lhsT=wo_codes[:].bitcast(FP8X4), lhsT_scale=wo_scales[:],
+                            rhs=dy_codes[:].bitcast(FP8X4), rhs_scale=dy_scales[:], start=True, stop=True)
         lns = held("lns", M, F32, DY_AT + 6 * M)
         nc.scalar.activation(lns[:], s[:], ACT.Ln, bias=1.0)
         rec = sb.tile([P, M], F32, name="rec")
-        nc.scalar.activation(rec[:], lns[:], ACT.Exp, scale=-1.0)
-        xg1 = held("xg1", J, BF16, S_AT)
-        nc.vector.tensor_copy(xg1[:], x_win[1][:].indirect(idx[:]))
-        cg4 = held("cg4", M, F32, X1_AT)
+        nc.scalar.activation(rec[:], lns[:], ACT.Exp, scale=-1.0, bias=math.log(0.5))
+        xg2 = held("xg2", J, BF16, EZ_AT - 2 * J)
+        nc.vector.tensor_copy(xg2[:], x_win[2][:].indirect(idx[:]))
+        cg4 = held("cg4", M, F32, X2_AT)
         nc.vector.tensor_tensor(cg4[:], c0[:], g4[:], ALU.mult)
-        q3 = held("q3", M, F32, PLACED_AT - 4 * M)
+        q3 = held("q3", M, F32, X2_AT + 4 * M)
         nc.vector.tensor_tensor(q3[:], c0[:], p23[:], ALU.mult)
         q1 = sb.tile([P, M], F32, name="q1")
         nc.vector.tensor_tensor(q1[:], cg4[:], g3[:], ALU.mult)
@@ -168,16 +175,17 @@ def tile_attend_ctriples_w_kernel(tc, tab_words, tab_scales, w1, bias, wo, dy, j
 
         th = held("th", J, F32, DY_AT)
         for u in range(2):
-            nc.scalar.activation(th[:, u * HALF:(u + 1) * HALF], a_ps[u][:], ACT.Tanh, bias=half_b[:], scale=0.5)
+            nc.scalar.activation(th[:].rearrange("r (t p) -> r t p", t=PACK)[:, :, u * P // 2:(u + 1) * P // 2],
+                                 a_ps[u][:].rearrange("r (p t) -> r t p", t=PACK), ACT.Tanh, bias=half_b[:], scale=0.5)
         th_ps = ps.tile([P, PACK, R], F32, name="th_ps", tag="turned")
         for t in range(PACK):
-            nc.tensor.transpose(th_ps[:, t, :], th[:, t:J:PACK], ident[:])
-        mid = held("mid", 2 * J, BF16, DY_AT + 8 * M)
-        turn_x(xg1, ps.tile([P, 2, P], F32, name="x_ps1", tag="x_ps"), mid[:, 0:J])
+            nc.tensor.transpose(th_ps[:, t, :], th[:, t * P:(t + 1) * P], ident[:])
+        xt2 = sb.tile([P, J], BF16, name="xt2", align_bytes=64)
+        turn_x(xg2, ps.tile([P, 2, P], F32, name="x_ps2", tag="a0"), xt2[:])
         sj = sb.tile([P, PACK, R], F32, name="sj")
         for t in range(PACK):
             nc.scalar.activation(sj[:, t, :], th_ps[:, t, :], ACT.Identity,
-                                 bias=half_js[:, t:t + 1], scale=half_js[:, t:t + 1])
+                                 bias=js_col[:, t:t + 1], scale=js_col[:, t:t + 1])
         x3_bf = held("x3_bf", T, BF16, JS_AT)
         nc.scalar.activation(x3_bf[:], x_win[3][:], ACT.Copy)
 
@@ -187,25 +195,25 @@ def tile_attend_ctriples_w_kernel(tc, tab_words, tab_scales, w1, bias, wo, dy, j
             for t in range(PACK):
                 nc.tensor.matmul(dh_ps[:, t, :], lhsT=win[:, t:J:PACK], rhs=ident[:], is_transpose=True,
                                  start=(n == 0 and t == 0), stop=(n == 2 and t == PACK - 1))
+        x01_scales = held("x01_scales", 2 * P, U8, PLACED_AT)
+        x01_codes = quantize("x01_codes", xt01[:], x01_scales)
+        x2_scales = held("x2_scales", P, U8, PLACED_AT + 2 * P)
+        x2_codes = quantize("x2_codes", xt2[:], x2_scales)
         xg3 = held("xg3", J, BF16, PLACED_AT + 2 * J)
         nc.scalar.activation(xg3[:], x3_bf[:].indirect(idx[:]), ACT.Copy)
-        turn_x(xg3, ps.tile([P, 2, P], F32, name="x_ps3"), mid[:, J:2 * J])
-        xg2 = held("xg2", J, BF16, PLACED_AT - J)
-        nc.vector.tensor_copy(xg2[:], x_win[2][:].indirect(idx[:]))
-        xt2 = held("xt2", J, BF16, JS_AT)
-        turn_x(xg2, ps.tile([P, 2, P], F32, name="x_ps2", tag="x_ps"), xt2[:])
+        xt3 = sb.tile([P, J], BF16, name="xt3", align_bytes=64)
+        turn_x(xg3, ps.tile([P, 2, P], F32, name="x_ps3", tag="x_ps"), xt3[:])
 
-        gs = sb.tile([P, R * PACK], BF16, name="gs", tag="x2", align_bytes=64)
+        gs = sb.tile([P, J], BF16, name="gs", align_bytes=64)
         nc.vector.tensor_tensor(gs[:].rearrange("p (c i t) -> p c t i", i=4, t=PACK),
                                 dh_ps[:].rearrange("p t (c i) -> p c t i", i=4),
                                 sj[:].rearrange("p t (c i) -> p c t i", i=4), ALU.mult)
-        late = {}
-        for name, src in (("mid", mid), ("g", gs), ("x2", xt2)):
-            scales = sb.tile([P, src.shape[1] // PACK], U8, name=name + "_scales", align_bytes=64)
-            late[name] = (quantize(name + "_codes", src[:], scales)[:], scales[:])
-        xq = [(early_codes[:, 0:P], early_scales[:, 0:P]), (late["mid"][0][:, 0:P], late["mid"][1][:, 0:P]), late["x2"],
-              (late["mid"][0][:, P:2 * P], late["mid"][1][:, P:2 * P])]
-        g_codes, g_scales = late["g"]
+        g_scales = sb.tile([P, R], U8, name="g_scales", align_bytes=64)
+        g_codes = quantize("g_codes", gs[:], g_scales)
+        x3_scales = sb.tile([P, P], U8, name="x3_scales", align_bytes=64)
+        x3_codes = quantize("x3_codes", xt3[:], x3_scales)
+        xq = [(x01_codes[:, 0:P], x01_scales[:, 0:P]), (x01_codes[:, P:2 * P], x01_scales[:, P:2 * P]),
+              (x2_codes[:], x2_scales[:]), (x3_codes[:], x3_scales[:])]
         res = sb.tile([P, PACK * R], F32, name="res")
         out_rows = out.rearrange("(p c) r -> p (c r)", c=PACK)
         for u, queue in enumerate((nc.sync, nc.scalar)):
@@ -213,7 +221,7 @@ def tile_attend_ctriples_w_kernel(tc, tab_words, tab_scales, w1, bias, wo, dy, j
             for c in range(2):
                 codes, scales = xq[2 * u + c]
                 nc.tensor.matmul_mx(out=gw[:, c * R:(c + 1) * R], lhsT=codes.bitcast(FP8X4), lhsT_scale=scales,
-                                    rhs=g_codes.bitcast(FP8X4), rhs_scale=g_scales, start=True, stop=True)
+                                    rhs=g_codes[:].bitcast(FP8X4), rhs_scale=g_scales[:], start=True, stop=True)
             cols = slice(u * 2 * R, (u + 1) * 2 * R)
             nc.vector.tensor_tensor(res[:, cols], gw[:], old_sb[:, cols], ALU.add)
             queue.dma_start(out_rows[:, cols], res[:, cols])

@@ -86,7 +86,7 @@ def tile_attend_ctriples_w_kernel(tc, tab_words, tab_scales, w1, bias, wo, dy, j
         nc.sync.dma_start(dy_raw[:], dy.rearrange("(p t) m -> p t m", t=PACK))
         wo_raw = sb.tile([P, PACK, R], F32, name="wo_raw", tag="wo", align_bytes=64)
         nc.sync.dma_start(wo_raw[:], wo.rearrange("(p t) r -> p t r", t=PACK))
-        js_col = held("js_col", PACK, F32, JS_AT)
+        js_col = sb.tile([P, PACK], F32, name="js_col")
         nc.sync.dma_start(js_col[:], js.rearrange("o (p t) -> (o p) t", t=PACK))
         nc.sync.dma_start(x_win[2][:], x_rows[:, 2, :])
         nc.sync.dma_start(x_win[3][:], x_rows[:, 3, :])
@@ -99,7 +99,7 @@ def tile_attend_ctriples_w_kernel(tc, tab_words, tab_scales, w1, bias, wo, dy, j
                   sb.tile([P, J], F32, name="placed2")]
         for win in placed:
             nc.vector.memset(win[:], 0.0)
-        half_b = sb.tile([P, 1], F32, name="half_b")
+        half_b = held("half_b", 1, F32, JS_AT)
         nc.gpsimd.tensor_scalar(half_b[:], b_col[:], 0.5, 0.0, ALU.mult, ALU.add)
 
         w1_bf = sb.tile([P, R * PACK], BF16, name="w1_bf", align_bytes=64)
@@ -142,7 +142,7 @@ def tile_attend_ctriples_w_kernel(tc, tab_words, tab_scales, w1, bias, wo, dy, j
         interleave(wo_bf[:], wo_raw)
         xt01 = sb.tile([P, 2 * J], BF16, name="xt01", tag="wo", align_bytes=64)
         turn_x(xg0, ps.tile([P, 2, P], F32, name="x_ps0", tag="x_ps"), xt01[:, 0:J])
-        turn_x(xg1, ps.tile([P, 2, P], F32, name="x_ps1"), xt01[:, J:2 * J])
+        turn_x(xg1, ps.tile([P, 2, P], F32, name="x_ps1", tag="x_ps1"), xt01[:, J:2 * J])
 
         g2, g3, g4 = (sb.tile([P, M], F32, name=f"g{n}") for n in (2, 3, 4))
         for g, lst in zip((g2, g3, g4), lists):
@@ -177,19 +177,19 @@ def tile_attend_ctriples_w_kernel(tc, tab_words, tab_scales, w1, bias, wo, dy, j
         for u in range(2):
             nc.scalar.activation(th[:].rearrange("r (t p) -> r t p", t=PACK)[:, :, u * P // 2:(u + 1) * P // 2],
                                  a_ps[u][:].rearrange("r (p t) -> r t p", t=PACK), ACT.Tanh, bias=half_b[:], scale=0.5)
-        th_ps = ps.tile([P, PACK, R], F32, name="th_ps", tag="turned")
+        th_ps = ps.tile([P, PACK, R], F32, name="th_ps")
         for t in range(PACK):
             nc.tensor.transpose(th_ps[:, t, :], th[:, t * P:(t + 1) * P], ident[:])
-        xt2 = sb.tile([P, J], BF16, name="xt2", align_bytes=64)
-        turn_x(xg2, ps.tile([P, 2, P], F32, name="x_ps2", tag="a0"), xt2[:])
+        xt2 = held("xt2", J, BF16, DY_AT + 8 * M)
+        turn_x(xg2, ps.tile([P, 2, P], F32, name="x_ps2", tag="x_ps1"), xt2[:])
+        x3_bf = held("x3_bf", T, BF16, JS_AT)
+        nc.scalar.activation(x3_bf[:], x_win[3][:], ACT.Copy)
         sj = sb.tile([P, PACK, R], F32, name="sj")
         for t in range(PACK):
             nc.scalar.activation(sj[:, t, :], th_ps[:, t, :], ACT.Identity,
                                  bias=js_col[:, t:t + 1], scale=js_col[:, t:t + 1])
-        x3_bf = held("x3_bf", T, BF16, JS_AT)
-        nc.scalar.activation(x3_bf[:], x_win[3][:], ACT.Copy)
 
-        dh_ps = ps.tile([P, PACK, R], F32, name="dh_ps", tag="turned")
+        dh_ps = ps.tile([P, PACK, R], F32, name="dh_ps", tag="x_ps1")
         for n, (win, lst, qn) in enumerate(zip(placed, lists, (q1, q2, q3))):
             nc.vector.tensor_tensor(win[:].indirect(lst[:]), qn[:], rec[:], ALU.mult)
             for t in range(PACK):
@@ -199,7 +199,7 @@ def tile_attend_ctriples_w_kernel(tc, tab_words, tab_scales, w1, bias, wo, dy, j
         x01_codes = quantize("x01_codes", xt01[:], x01_scales)
         x2_scales = held("x2_scales", P, U8, PLACED_AT + 2 * P)
         x2_codes = quantize("x2_codes", xt2[:], x2_scales)
-        xg3 = held("xg3", J, BF16, PLACED_AT + 2 * J)
+        xg3 = sb.tile([P, J], BF16, name="xg3", align_bytes=64)
         nc.scalar.activation(xg3[:], x3_bf[:].indirect(idx[:]), ACT.Copy)
         xt3 = sb.tile([P, J], BF16, name="xt3", align_bytes=64)
         turn_x(xg3, ps.tile([P, 2, P], F32, name="x_ps3", tag="x_ps"), xt3[:])

import math
from contextlib import ExitStack

import concourse.mybir as mybir
from concourse.masks import make_identity

K, R, F, T, J, M = 512, 128, 512, 2048, 512, 256
FLOPS = 2 * K * R * J + 2 * F * R * M + 2 * J * K * R

F32 = mybir.dt.float32
BF16 = mybir.dt.bfloat16
I32 = mybir.dt.int32
U32 = mybir.dt.uint32
U16 = mybir.dt.uint16
U8 = mybir.dt.uint8
FP8X4 = mybir.dt.float8_e4m3fn_x4
FP4X4 = mybir.dt.float4_e2m1fn_x4
ACT = mybir.ActivationFunctionType
ALU = mybir.AluOpType

P = 128
PACK = 4
HALF = J // 2
EZ_AT = 2 * J
PLACED_AT = EZ_AT + 4 * J
JS_AT = PLACED_AT + 4 * J
DY_AT = JS_AT + 2 * T
X0_AT = DY_AT + 16 * M
MAG_AT = X0_AT + 4 * T
POS_AT = MAG_AT - 2 * J
SOFT_AT = MAG_AT + 2 * J
H_AT = SOFT_AT + 4 * J
X2_AT = H_AT + 4 * T


def tile_attend_ctriples_w_kernel(tc, tab_words, tab_scales, w1, bias, wo, dy, js, xrows, old,
                                   offs, offs2, offs3, offs4, out):
    nc = tc.nc
    with ExitStack() as ctx:
        sb = ctx.enter_context(tc.tile_pool(name="sb", bufs=1))
        hold = ctx.enter_context(tc.tile_pool(name="hold", bufs=1))
        ps = ctx.enter_context(tc.psum_pool(name="ps", bufs=1))

        def held(name, width, dtype, at):
            return hold.tile([P, width], dtype, name=name, offset=at, align_bytes=64)

        def quantize(name, src, scales):
            codes = sb.tile([P, src.shape[1] // PACK], U32, name=name, align_bytes=64)
            nc.vector.quantize_mx(out=codes[:].bitcast(FP8X4), scales=scales[:], in_=src)
            return codes

        def interleave(grouped, raw):
            nc.scalar.activation(grouped.rearrange("p (c i t) -> p c t i", i=4, t=PACK),
                                 raw[:].rearrange("p t (c i) -> p c t i", i=4), ACT.Copy)

        def turn_x(xg, bank, xt):
            pairs = xg[:].bitcast(F32)
            for u in range(2):
                nc.tensor.transpose(bank[:, u, :], pairs[:, u:J // 2:2], ident[:])
            nc.scalar.copy(xt.bitcast(F32).rearrange("p (k u) -> p k u", u=2), bank[:].rearrange("p u k -> p k u"))

        idx = sb.tile([P, J // 16], U16, name="idx")
        nc.sync.dma_start(idx[:], offs)
        words = sb.tile([P, T], U16, name="words", align_bytes=64)
        nc.sync.dma_start(words[:].bitcast(I32), tab_words[0].bitcast(I32))
        b_col = sb.tile([P, 1], F32, name="b_col")
        nc.sync.dma_start(b_col[:], bias)
        w1_raw = sb.tile([P, PACK, R], F32, name="w1_raw")
        nc.sync.dma_start(w1_raw[:], w1.rearrange("(p t) r -> p t r", t=PACK))
        sbytes = sb.tile([P, T], U8, name="sbytes", align_bytes=64)
        nc.gpsimd.memset(sbytes[:].bitcast(I32), 0)
        for q in range(4):
            nc.sync.dma_start(sbytes[32 * q:32 * q + 4, :].bitcast(I32),
                              tab_scales[0, 4 * q:4 * q + 4, :].bitcast(I32))
        x_rows = xrows.rearrange("(p c) t -> p c t", c=PACK)
        x_win = [held("x_win0", T, F32, X0_AT), held("x_win1", T, F32, H_AT),
                 held("x_win2", T, F32, X2_AT), sb.tile([P, T], F32, name="x_win3")]
        nc.sync.dma_start(x_win[0][:], x_rows[:, 0, :])
        nc.sync.dma_start(x_win[1][:], x_rows[:, 1, :])
        lists = []
        for n, src in enumerate((offs2, offs3, offs4)):
            lst = sb.tile([P, M // 16], U16, name=f"idx{n + 2}")
            nc.sync.dma_start(lst[:], src)
            lists.append(lst)
        dy_raw = hold.tile([P, PACK, M], F32, name="dy_raw", offset=DY_AT, align_bytes=64)
        nc.sync.dma_start(dy_raw[:], dy.rearrange("(p t) m -> p t m", t=PACK))
        wo_raw = sb.tile([P, PACK, R], F32, name="wo_raw", tag="wo", align_bytes=64)
        nc.sync.dma_start(wo_raw[:], wo.rearrange("(p t) r -> p t r", t=PACK))
        js_col = sb.tile([P, PACK], F32, name="js_col")
        nc.sync.dma_start(js_col[:], js.rearrange("o (p t) -> (o p) t", t=PACK))
        nc.sync.dma_start(x_win[2][:], x_rows[:, 2, :])
        nc.sync.dma_start(x_win[3][:], x_rows[:, 3, :])
        old_sb = sb.tile([P, PACK * R], F32, name="old_sb")
        nc.sync.dma_start(old_sb[:], old.rearrange("(p c) r -> p (c r)", c=PACK))

        ident = sb.tile([P, P], F32, name="ident")
        make_identity(nc, ident[:])
        placed = [sb.tile([P, J], F32, name="placed0"), held("placed1", J, F32, PLACED_AT),
                  sb.tile([P, J], F32, name="placed2")]
        for win in placed:
            nc.vector.memset(win[:], 0.0)
        half_b = held("half_b", 1, F32, JS_AT)
        nc.gpsimd.tensor_scalar(half_b[:], b_col[:], 0.5, 0.0, ALU.mult, ALU.add)

        w1_bf = sb.tile([P, R * PACK], BF16, name="w1_bf", align_bytes=64)
        interleave(w1_bf[:], w1_raw)
        tab_w = sb.tile([P, J], U16, name="tab_w", align_bytes=64)
        nc.vector.tensor_copy(tab_w[:], words[:].indirect(idx[:]))
        w1_scales = sb.tile([P, R], U8, name="w1_scales", align_bytes=64)
        w1_codes = quantize("w1_codes", w1_bf[:], w1_scales)
        a_ps = []
        ez = held("ez", J, F32, EZ_AT)
        mag = held("mag", J, F32, MAG_AT)
        halves = [slice(u * HALF, (u + 1) * HALF) for u in range(2)]
        for u in range(2):
            tab_s = sb.tile([P, HALF], U8, name=f"tab_s{u}", align_bytes=64)
            nc.vector.tensor_copy(tab_s[:], sbytes[:].indirect(idx[:, u * HALF // 16:(u + 1) * HALF // 16]))
            acc = ps.tile([P, HALF], F32, name=f"a_ps{u}", tag=f"a{u}")
            nc.tensor.matmul_mx(out=acc[:], lhsT=w1_codes[:].bitcast(FP8X4), lhsT_scale=w1_scales[:],
                                rhs=tab_w[:, u * HALF:(u + 1) * HALF].bitcast(FP4X4), rhs_scale=tab_s[:],
                                start=True, stop=True)
            a_ps.append(acc)
            nc.scalar.activation(mag[:, halves[u]], acc[:], ACT.Abs, bias=b_col[:])
            nc.scalar.activation(ez[:, halves[u]], mag[:, halves[u]], ACT.Exp, scale=-1.0)

        xg0 = sb.tile([P, J], BF16, name="xg0", align_bytes=64)
        nc.vector.tensor_copy(xg0[:], x_win[0][:].indirect(idx[:]))
        pos = held("pos", J, F32, POS_AT)
        for u in range(2):
            nc.vector.tensor_scalar(pos[:, halves[u]], a_ps[u][:], b_col[:], 0.0, ALU.add, ALU.max)
        xg1 = sb.tile([P, J], BF16, name="xg1", align_bytes=64)
        nc.vector.tensor_copy(xg1[:], x_win[1][:].indirect(idx[:]))
        h = held("h", J, F32, H_AT)
        soft = held("soft", J, F32, SOFT_AT)
        for u in range(2):
            nc.scalar.activation(soft[:, halves[u]], ez[:, halves[u]], ACT.Ln, bias=1.0)
            nc.vector.tensor_tensor(h[:, halves[u]], soft[:, halves[u]], pos[:, halves[u]], ALU.add)

        dy_bf = held("dy_bf", 2 * J, BF16, EZ_AT - 2 * J)
        interleave(dy_bf[:], dy_raw)
        wo_bf = held("wo_bf", J, BF16, EZ_AT + 2 * J)
        interleave(wo_bf[:], wo_raw)
        xt01 = sb.tile([P, 2 * J], BF16, name="xt01", tag="wo", align_bytes=64)
        turn_x(xg0, ps.tile([P, 2, P], F32, name="x_ps0", tag="x_ps"), xt01[:, 0:J])
        turn_x(xg1, ps.tile([P, 2, P], F32, name="x_ps1", tag="x_ps1"), xt01[:, J:2 * J])

        g2, g3, g4 = (sb.tile([P, M], F32, name=f"g{n}") for n in (2, 3, 4))
        for g, lst in zip((g2, g3, g4), lists):
            nc.vector.tensor_copy(g[:], h[:].indirect(lst[:]))
        p23 = sb.tile([P, M], F32, name="p23")
        nc.vector.tensor_tensor(p23[:], g2[:], g3[:], ALU.mult)
        dy_scales = held("dy_scales", M, U8, H_AT)
        dy_codes = quantize("dy_codes", dy_bf[:], dy_scales)
        s = sb.tile([P, M], F32, name="s")
        nc.vector.tensor_tensor(s[:], p23[:], g4[:], ALU.mult)
        wo_scales = held("wo_scales", R, U8, EZ_AT)
        wo_codes = quantize("wo_codes", wo_bf[:], wo_scales)
        c0 = ps.tile([P, M], F32, name="c0")
        nc.tensor.matmul_mx(out=c0[:], lhsT=wo_codes[:].bitcast(FP8X4), lhsT_scale=wo_scales[:],
                            rhs=dy_codes[:].bitcast(FP8X4), rhs_scale=dy_scales[:], start=True, stop=True)
        lns = held("lns", M, F32, DY_AT + 6 * M)
        nc.scalar.activation(lns[:], s[:], ACT.Ln, bias=1.0)
        rec = sb.tile([P, M], F32, name="rec")
        nc.scalar.activation(rec[:], lns[:], ACT.Exp, scale=-1.0, bias=math.log(0.5))
        xg2 = held("xg2", J, BF16, EZ_AT - 2 * J)
        nc.vector.tensor_copy(xg2[:], x_win[2][:].indirect(idx[:]))
        cg4 = held("cg4", M, F32, X2_AT)
        nc.vector.tensor_tensor(cg4[:], c0[:], g4[:], ALU.mult)
        q3 = held("q3", M, F32, X2_AT + 4 * M)
        nc.vector.tensor_tensor(q3[:], c0[:], p23[:], ALU.mult)
        q1 = sb.tile([P, M], F32, name="q1")
        nc.vector.tensor_tensor(q1[:], cg4[:], g3[:], ALU.mult)
        q2 = sb.tile([P, M], F32, name="q2")
        nc.vector.tensor_tensor(q2[:], cg4[:], g2[:], ALU.mult)

        th = held("th", J, F32, DY_AT)
        for u in range(2):
            nc.scalar.activation(th[:].rearrange("r (t p) -> r t p", t=PACK)[:, :, u * P // 2:(u + 1) * P // 2],
                                 a_ps[u][:].rearrange("r (p t) -> r t p", t=PACK), ACT.Tanh, bias=half_b[:], scale=0.5)
        th_ps = ps.tile([P, PACK, R], F32, name="th_ps")
        for t in range(PACK):
            nc.tensor.transpose(th_ps[:, t, :], th[:, t * P:(t + 1) * P], ident[:])
        xt2 = held("xt2", J, BF16, DY_AT + 8 * M)
        turn_x(xg2, ps.tile([P, 2, P], F32, name="x_ps2", tag="x_ps1"), xt2[:])
        x3_bf = held("x3_bf", T, BF16, JS_AT)
        nc.scalar.activation(x3_bf[:], x_win[3][:], ACT.Copy)
        sj = sb.tile([P, PACK, R], F32, name="sj")
        for t in range(PACK):
            nc.scalar.activation(sj[:, t, :], th_ps[:, t, :], ACT.Identity,
                                 bias=js_col[:, t:t + 1], scale=js_col[:, t:t + 1])

        dh_ps = ps.tile([P, PACK, R], F32, name="dh_ps", tag="x_ps1")
        for n, (win, lst, qn) in enumerate(zip(placed, lists, (q1, q2, q3))):
            nc.vector.tensor_tensor(win[:].indirect(lst[:]), qn[:], rec[:], ALU.mult)
            for t in range(PACK):
                nc.tensor.matmul(dh_ps[:, t, :], lhsT=win[:, t:J:PACK], rhs=ident[:], is_transpose=True,
                                 start=(n == 0 and t == 0), stop=(n == 2 and t == PACK - 1))
        x01_scales = held("x01_scales", 2 * P, U8, PLACED_AT)
        x01_codes = quantize("x01_codes", xt01[:], x01_scales)
        x2_scales = held("x2_scales", P, U8, PLACED_AT + 2 * P)
        x2_codes = quantize("x2_codes", xt2[:], x2_scales)
        xg3 = sb.tile([P, J], BF16, name="xg3", align_bytes=64)
        nc.scalar.activation(xg3[:], x3_bf[:].indirect(idx[:]), ACT.Copy)
        xt3 = sb.tile([P, J], BF16, name="xt3", align_bytes=64)
        turn_x(xg3, ps.tile([P, 2, P], F32, name="x_ps3", tag="x_ps"), xt3[:])

        gs = sb.tile([P, J], BF16, name="gs", align_bytes=64)
        nc.vector.tensor_tensor(gs[:].rearrange("p (c i t) -> p c t i", i=4, t=PACK),
                                dh_ps[:].rearrange("p t (c i) -> p c t i", i=4),
                                sj[:].rearrange("p t (c i) -> p c t i", i=4), ALU.mult)
        g_scales = sb.tile([P, R], U8, name="g_scales", align_bytes=64)
        g_codes = quantize("g_codes", gs[:], g_scales)
        x3_scales = sb.tile([P, P], U8, name="x3_scales", align_bytes=64)
        x3_codes = quantize("x3_codes", xt3[:], x3_scales)
        xq = [(x01_codes[:, 0:P], x01_scales[:, 0:P]), (x01_codes[:, P:2 * P], x01_scales[:, P:2 * P]),
              (x2_codes[:], x2_scales[:]), (x3_codes[:], x3_scales[:])]
        res = sb.tile([P, PACK * R], F32, name="res")
        out_rows = out.rearrange("(p c) r -> p (c r)", c=PACK)
        for u, queue in enumerate((nc.sync, nc.scalar)):
            gw = ps.tile([P, 2 * R], F32, name=f"gw{u}")
            for c in range(2):
                codes, scales = xq[2 * u + c]
                nc.tensor.matmul_mx(out=gw[:, c * R:(c + 1) * R], lhsT=codes.bitcast(FP8X4), lhsT_scale=scales,
                                    rhs=g_codes[:].bitcast(FP8X4), rhs_scale=g_scales[:], start=True, stop=True)
            cols = slice(u * 2 * R, (u + 1) * 2 * R)
            nc.vector.tensor_tensor(res[:, cols], gw[:], old_sb[:, cols], ALU.add)
            queue.dma_start(out_rows[:, cols], res[:, cols])
